import numpy as np, ml_dtypes
CORES = [8,9,10,11,12,13]
N = 6
import mx_ref
BF = ml_dtypes.bfloat16
def gentries(a):
    return np.ascontiguousarray(a.reshape(8, 16, -1).transpose(0, 2, 1)).reshape(8, -1)
def gtable(e):
    e = np.asarray(e); return np.ascontiguousarray(e.reshape(8, -1, 16).transpose(0, 2, 1)).reshape(128, -1).astype(np.int32)
def gcols(t, e):
    v = np.concatenate([t.reshape(8, 16, -1, 4), np.zeros((8, 16, 1, 4), BF)], axis=2)
    return np.ascontiguousarray(np.stack([v[g][:, e[g]] for g in range(8)])).reshape(128, -1)
def f(rng, *shape):
    return mx_ref.flush((rng.standard_normal(shape, dtype=np.float32) * np.exp2(rng.integers(-2, 3, shape[:-1] + (1,)))).astype(BF))
def wide(rng, *shape, cols=0):
    v = rng.standard_normal(shape, dtype=np.float32) * np.exp2(rng.integers(-12, 13, shape)).astype(np.float32)
    if cols: v *= np.repeat(np.exp2(rng.integers(-cols, cols + 1, shape[:-2] + (1, shape[-1] // 4))) * (rng.random(shape[:-2] + (1, shape[-1] // 4)) > 0.0625), 4, axis=-1).astype(np.float32)
    return mx_ref.flush(v.astype(BF))
S = 128
def block(rng, how):
    if how == "one": return np.full((8, S), rng.integers(0, 128))
    if how == "groups": return np.tile(rng.integers(0, 128, S), (8, 1))
    if how == "ends": return np.stack([rng.permutation(np.arange(S) % 2 * 127) for g in range(8)])
    if how == "distinct": return np.stack([np.tile(rng.permutation(128), S // 128) for g in range(8)])
    return rng.integers(0, 128, (8, S))
def lists(rng, how=""):
    return {"cw": np.stack([gtable(np.concatenate([block(rng, how) for s in range(N)], axis=1)) for r in range(N)])}
def setup_inputs(rng):
    return {"bk": f(rng, N, 128, 512), "x": f(rng, N, 128, 512 * N), **lists(rng)}
def setup_inputs_one(rng):
    return {**setup_inputs(rng), **lists(rng, "one")}
def setup_inputs_groups(rng):
    return {**setup_inputs(rng), **lists(rng, "groups")}
def setup_inputs_ends(rng):
    return {**setup_inputs(rng), **lists(rng, "ends")}
def setup_inputs_distinct(rng):
    return {**setup_inputs(rng), **lists(rng, "distinct")}
def setup_inputs_spread(rng):
    d = setup_inputs(rng); d["bk"] = wide(rng, N, 128, 512, cols=4); d["x"] = wide(rng, N, 128, 512 * N); return d
def check_inputs(d):
    b = []
    for r in range(N):
        e = d["cw"][r]
        if e.min() < 0 or e.max() > 127: b.append("cw")
    return b
def reference(bk, x, cw):
    y = np.zeros((N, 128, S), np.float32)
    for r in range(N):
        e = gentries(cw[r])
        for s in range(N):
            W = gcols(bk[s], e[:, S * s:S * s + S])
            X = np.ascontiguousarray(x[r][:, 512 * s:512 * s + 512])
            y[r] += mx_ref.matmul(mx_ref.quantize(X), mx_ref.quantize(W))
    return {"y": y}

@@ -1,0 +1,234 @@
+from concourse.bass import DstId, RemoteDMATransfer
+from concourse.mybir import dt, ActivationFunctionType
+
+N = 6
+S = 128
+L = S // 16
+CFG = dict(cols=[(2, 0), (1, 0), (2, 1), (1, 1), (0, 1)], rounds=[1, 2, 1, 1], vs=[2, 2, 2, 1], ahead=[1, 0, 0, 0],
+           sends=[1, 1, 1, 1, 1], sc=[[0], [], [1, 2], [3], [4]], lc=[1, 2, 2], e1=8, xl=[3, 3], xq=[2, 2, 2], nl=1, nq=1,
+           go=2)
+
+SCRATCH = {
+    "cwi": ("sbuf", [128, N * L], "int32"),
+    "lu": ("sbuf", [128, N * L], "uint16"),
+    "off": ("sbuf", [128, (N - 1) * L], "uint16"),
+    "bks": ("sbuf", [128, 4 * S], "bfloat16"),
+    "win": ("sbuf", [128, 4 * S], "bfloat16"),
+    "h": ("sbuf", [128, 4 * S * (N - 1)], "bfloat16"),
+    "ho": ("sbuf", [128, 4 * S], "bfloat16"),
+    "xs": ("sbuf", [128, 4 * S * N], "bfloat16"),
+    "sq": ("sbuf", [128, S * (N - 1)], "float8_e4m3fn_x4"),
+    "ss": ("sbuf", [128, S * (N - 1)], "uint8"),
+    "oq": ("sbuf", [128, S], "float8_e4m3fn_x4"),
+    "osc": ("sbuf", [128, S], "uint8"),
+    "rq": ("sbuf", [128, S * N], "float8_e4m3fn_x4"),
+    "rs": ("sbuf", [128, S * N], "uint8"),
+    "xq": ("sbuf", [128, S * N], "float8_e4m3fn_x4"),
+    "xsc": ("sbuf", [128, S * N], "uint8"),
+    "yo": ("sbuf", [128, S], "float32"),
+    "ps": ("psum", [128, 512], "float32"),
+}
+SEMAPHORES = (["ld_cw", "ld_bk", "cast", "go", "winv", "wins", "ownv", "owns", "ownq", "mm", "yc", "st", "sent"]
+              + ["ld_x%d" % k for k in range(N)] + ["xqd%d" % k for k in range(N)]
+              + ["lst%d" % k for k in range(N)] + ["arr%d" % k for k in range(N)]
+              + ["gv%d" % k for k in range(N)] + ["gs%d" % k for k in range(N)] + ["qd%d" % k for k in range(N)])
+
+
+def edges(ns):
+    return [(sum(ns[:i]), sum(ns[:i + 1])) for i in range(len(ns))]
+
+
+def serves(s):
+    return [2 * ((s // 2 + d) % (N // 2)) + (s + f) % 2 for d, f in CFG["cols"]]
+
+
+def split(engs, k):
+    if k == 3:
+        return [engs[0::4], engs[2::4], engs[1::2]]
+    return [engs[i::k] for i in range(k)]
+
+
+def bits(es):
+    m = 0
+    for e in es:
+        m |= 1 << e
+    return m
+
+
+def rank_program(g, core, T, topo):
+    rank = T.rank_of(core)
+    if rank is None:
+        return
+    cores = T.cores
+    sem = T.sem
+    v, a, te, sy = g.vector, g.scalar, g.tensor, g.sync
+    COPY = ActivationFunctionType.Copy
+
+    rounds, sends, lists = edges(CFG["rounds"]), edges(CFG["sends"]), edges(CFG["lc"])
+    codes, scales = [list(range(i, j)) for i, j in sends], CFG["sc"]
+    xl, xq = edges(CFG["xl"]), edges(CFG["xq"])
+    mine = serves(rank)
+
+    def dst(r):
+        rid, pid, _ = topo.addr(cores[r])
+        return DstId(rid=rid, pnc=pid)
+
+    def place(s, r):
+        return serves(s).index(r)
+
+    servers = sorted([s for s in range(N) if s != rank], key=lambda s: place(s, rank))
+    engs = topo.engines(core, cores[mine[0]])
+
+    def list_engs(c, n):
+        return split(engs[::len(engs) // CFG["e1"]] if c == 0 else engs, n)
+
+    def list_count(k):
+        for c, (i, j) in enumerate(lists):
+            if i <= k < j:
+                return len(list_engs(c, j - i)[k - i])
+
+    def arr_count(k):
+        return sum(len(split(engs, len(ks))[ks.index(k)]) for ks in codes + scales if k in ks)
+
+    left = [0]
+
+    def fused(parts):
+        tr = []
+        for r, src, dv, sm, es in parts:
+            tr.append(RemoteDMATransfer(dst_ids=[dst(r)], dma_engine_mask=bits(es), remote_sem=sm, src=src, dst=dv))
+            left[0] += len(es)
+        g.remote_dma_fused(tr, local_sem=sem.sent)
+
+    def load_x(i):
+        b0, b1 = 4 * S * xl[i][0], 4 * S * xl[i][1]
+        sy.dma_start(T.xs[:, b0:b1], T.x[:, b0:b1]).then_inc(sem["ld_x%d" % i], 16)
+
+    sy.dma_start(T.cwi[:], T.cw[:]).then_inc(sem.ld_cw, 16)
+    sy.dma_start(T.bks[:], T.bk[:]).then_inc(sem.ld_bk, 16)
+    for i in range(CFG["nl"]):
+        load_x(i)
+    sy.wait_ge(sem.go, 1)
+    for i in range(CFG["nl"], len(xl)):
+        load_x(i)
+
+    v.wait_ge(sem.ld_cw, 16)
+    v.tensor_copy(T.lu[:], T.cwi[:]).then_inc(sem.cast, 1)
+    g.wait_ge(sem.cast, 1)
+    for c, (i, j) in enumerate(lists):
+        es = list_engs(c, j - i)
+        parts = []
+        for k in range(i, j):
+            s = servers[k]
+            parts.append((s, T.lu[:, L * s:L * s + L], T.off[:, L * k:L * k + L], sem["lst%d" % k], es[k - i]))
+        fused(parts)
+        if c == CFG["go"]:
+            g.sem_inc(sem.go, 1)
+
+    def copy(q, o, i, sm):
+        if q is v:
+            v.tensor_copy(o, i).then_inc(sm, 1)
+        else:
+            a.activation(o, i, COPY).then_inc(sm, 1)
+
+    both = ((v, (0, 1)), (a, (2, 3)))
+    for q, ts in both:
+        q.wait_ge(sem.ld_bk, 16)
+        for t in ts:
+            copy(q, T.win[:, S * t:S * t + S], T.bks[:, t:4 * S:4], sem.winv if q is v else sem.wins)
+
+    def gather(q, t, buf, c0, n, offs, sm):
+        copy(q, buf[:, 4 * c0 + t:4 * (c0 + n):4], T.win[:, S * t:S * t + S].indirect(offs), sm)
+
+    own = T.lu[:, L * rank:L * rank + L]
+    v.wait_ge(sem.winv, 2)
+    v.wait_ge(sem.cast, 1)
+    a.wait_ge(sem.wins, 2)
+    a.wait_ge(sem.cast, 1)
+    for q, ts in both:
+        for t in ts:
+            gather(q, t, T.ho, 0, S, own, sem.ownv if q is v else sem.owns)
+    v.wait_ge(sem.ownv, 2)
+    v.wait_ge(sem.owns, 2)
+    v.quantize_mx(T.oq[:], T.osc[:], T.ho[:]).then_inc(sem.ownq, 1)
+
+    def quant_x(i):
+        for k in range(len(xl)):
+            if xl[k][0] < xq[i][1] and xq[i][0] < xl[k][1]:
+                v.wait_ge(sem["ld_x%d" % k], 16)
+        b0, b1 = S * xq[i][0], S * xq[i][1]
+        v.quantize_mx(T.xq[:, b0:b1], T.xsc[:, b0:b1], T.xs[:, 4 * b0:4 * b1]).then_inc(sem["xqd%d" % i], 1)
+
+    for i in range(CFG["nq"]):
+        quant_x(i)
+
+    def copies(q, i, ts):
+        k0, k1 = rounds[i]
+        for k in range(k0, k1):
+            q.wait_ge(sem["lst%d" % k], list_count(k))
+        for t in ts:
+            gather(q, t, T.h, S * k0, S * (k1 - k0), T.off[:, L * k0:L * k1], sem["gv%d" % i] if q is v else sem["gs%d" % i])
+
+    def send(ks, src, dv, coded):
+        es = split(engs, len(ks))
+        parts = []
+        for e, k in zip(es, ks):
+            x, z = src[:, S * k:S * k + S], dv[:, S * rank:S * rank + S]
+            if coded:
+                x, z = x.bitcast(dt.uint8), z.bitcast(dt.uint8)
+            parts.append((mine[k], x, z, sem["arr%d" % rank], e))
+        fused(parts)
+
+    a.wait_ge(sem.winv, 2)
+    v.wait_ge(sem.wins, 2)
+    begun = 0
+    for i, (k0, k1) in enumerate(rounds):
+        nv = CFG["vs"][i]
+        copies(a, i, range(nv, 4))
+        copies(v, i, range(begun, nv))
+        begun = CFG["ahead"][i]
+        if begun:
+            copies(v, i + 1, range(begun))
+        v.wait_ge(sem["gv%d" % i], nv)
+        v.wait_ge(sem["gs%d" % i], 4 - nv)
+        for m, (j0, j1) in enumerate(sends):
+            if not k0 <= j0 < k1:
+                continue
+            qd = sem["qd%d" % m]
+            c0, c1 = S * j0, S * j1
+            v.quantize_mx(T.sq[:, c0:c1], T.ss[:, c0:c1], T.h[:, 4 * c0:4 * c1]).then_inc(qd, 1)
+            g.wait_ge(qd, 1)
+            send(codes[m], T.sq, T.rq, True)
+            if scales[m]:
+                send(scales[m], T.ss, T.rs, False)
+
+    for i in range(CFG["nq"], len(xq)):
+        quant_x(i)
+
+    def tile(b, s):
+        return b[:, S * s:S * s + S]
+
+    def part(s):
+        return [p <= s < q for p, q in xq].index(True)
+
+    def arrival(s):
+        return [place(s, rank) in ks for ks in scales].index(True) if s != rank else 0
+
+    seq = sorted(range(N), key=lambda s: (arrival(s), part(s)))
+    for i, s in enumerate(seq):
+        te.wait_ge(sem["xqd%d" % part(s)], 1)
+        if s == rank:
+            te.wait_ge(sem.ownq, 1)
+            w, ws = T.oq[:], T.osc[:]
+        else:
+            te.wait_ge(sem["arr%d" % s], arr_count(place(s, rank)))
+            w, ws = tile(T.rq, s), tile(T.rs, s)
+        mm = te.matmul_mx(T.ps[:, 0:S], tile(T.xq, s), tile(T.xsc, s), w, ws, i == 0, i == N - 1)
+        if i == N - 1:
+            mm.then_inc(sem.mm, 1)
+
+    a.wait_ge(sem.mm, 1)
+    a.activation(T.yo[:], T.ps[:, 0:S], COPY).then_inc(sem.yc, 1)
+    a.wait_ge(sem.yc, 1)
+    a.dma_start(T.y[:], T.yo[:]).then_inc(sem.st, 16)
+    a.wait_ge(sem.st, 16)
+    g.wait_ge(sem.sent, left[0])

@@ -1,19 +1,28 @@
 from concourse.bass import DstId, RemoteDMATransfer
-from concourse.mybir import dt, ActivationFunctionType
+from concourse.mybir import dt, ActivationFunctionType, AluOpType
 
 N = 6
 S = 128
 L = S // 16
-CFG = dict(cols=[(2, 0), (1, 0), (2, 1), (1, 1), (0, 1)], rounds=[1, 2, 1, 1], vs=[2, 2, 2, 1], ahead=[1, 0, 0, 0],
-           sends=[1, 1, 1, 1, 1], sc=[[0], [], [1, 2], [3], [4]], lc=[1, 2, 2], e1=8, xl=[3, 3], xq=[2, 2, 2], nl=1, nq=1,
-           go=2)
+W = 2 * L
+U = 8
+CFG = dict(cols=[(2, 0), (1, 0), (2, 1), (1, 1), (0, 1)],
+           vec=[("a", 0, 8), ("a", 8, 16), ("q", 0), ("a", 16, 24), ("q", 1), ("a", 24, 30), ("q", 2),
+                ("a", 35, 40), ("q", 3), ("q", 4)],
+           sca=[("b", 0, 8), ("b", 8, 16), ("b", 16, 32), ("a", 30, 35), ("b", 32, 40)],
+           sc=[[0], [1], [2], [3], [4]], lc=[1, 2, 2], e1=8, xl=[4, 2], nl=1, nq=2, go=1)
 
 SCRATCH = {
-    "cwi": ("sbuf", [128, N * L], "int32"),
-    "lu": ("sbuf", [128, N * L], "uint16"),
-    "off": ("sbuf", [128, (N - 1) * L], "uint16"),
+    "cwi": ("sbuf", [128, 2, N * L], "int32"),
+    "pi": ("sbuf", [128, 1], "int32"),
+    "pj": ("sbuf", [128, 1], "int32"),
+    "par": ("sbuf", [128, 1], "float32"),
+    "l0": ("sbuf", [128, W], "uint16"),
+    "lo": ("sbuf", [128, W], "uint16"),
+    "lu": ("sbuf", [128, N, W], "uint16"),
+    "off": ("sbuf", [128, (N - 1) * W], "uint16"),
     "bks": ("sbuf", [128, 4 * S], "bfloat16"),
-    "win": ("sbuf", [128, 4 * S], "bfloat16"),
+    "odd": ("sbuf", [128, 4 * S], "bfloat16"),
     "h": ("sbuf", [128, 4 * S * (N - 1)], "bfloat16"),
     "ho": ("sbuf", [128, 4 * S], "bfloat16"),
     "xs": ("sbuf", [128, 4 * S * N], "bfloat16"),
@@ -28,10 +37,11 @@ SCRATCH = {
     "yo": ("sbuf", [128, S], "float32"),
     "ps": ("psum", [128, 512], "float32"),
 }
-SEMAPHORES = (["ld_cw", "ld_bk", "cast", "go", "winv", "wins", "ownv", "owns", "ownq", "mm", "yc", "st", "sent"]
+SEMAPHORES = (["ld_cw", "ld_bk", "iota", "par", "zero", "c0", "cast", "co", "go", "odd", "own", "ownq", "mm", "yc", "st",
+               "sent"]
               + ["ld_x%d" % k for k in range(N)] + ["xqd%d" % k for k in range(N)]
               + ["lst%d" % k for k in range(N)] + ["arr%d" % k for k in range(N)]
-              + ["gv%d" % k for k in range(N)] + ["gs%d" % k for k in range(N)] + ["qd%d" % k for k in range(N)])
+              + ["gv%d" % k for k in range(12)] + ["gs%d" % k for k in range(12)] + ["qd%d" % k for k in range(N)])
 
 
 def edges(ns):
@@ -64,9 +74,9 @@ def rank_program(g, core, T, topo):
     v, a, te, sy = g.vector, g.scalar, g.tensor, g.sync
     COPY = ActivationFunctionType.Copy
 
-    rounds, sends, lists = edges(CFG["rounds"]), edges(CFG["sends"]), edges(CFG["lc"])
-    codes, scales = [list(range(i, j)) for i, j in sends], CFG["sc"]
-    xl, xq = edges(CFG["xl"]), edges(CFG["xq"])
+    lists = edges(CFG["lc"])
+    codes, scales = [[k] for k in range(N - 1)], CFG["sc"]
+    xl = edges(CFG["xl"])
     mine = serves(rank)
 
     def dst(r):
@@ -103,7 +113,8 @@ def rank_program(g, core, T, topo):
         b0, b1 = 4 * S * xl[i][0], 4 * S * xl[i][1]
         sy.dma_start(T.xs[:, b0:b1], T.x[:, b0:b1]).then_inc(sem["ld_x%d" % i], 16)
 
-    sy.dma_start(T.cwi[:], T.cw[:]).then_inc(sem.ld_cw, 16)
+    sy.dma_start(T.cwi[0:128:2], T.cw[:]).then_inc(sem.ld_cw, 16)
+    a.dma_start(T.cwi[1:128:2], T.cw[:]).then_inc(sem.ld_cw, 16)
     sy.dma_start(T.bks[:], T.bk[:]).then_inc(sem.ld_bk, 16)
     for i in range(CFG["nl"]):
         load_x(i)
@@ -111,62 +122,68 @@ def rank_program(g, core, T, topo):
     for i in range(CFG["nl"], len(xl)):
         load_x(i)
 
-    v.wait_ge(sem.ld_cw, 16)
-    v.tensor_copy(T.lu[:], T.cwi[:]).then_inc(sem.cast, 1)
-    g.wait_ge(sem.cast, 1)
+    g.iota(T.pi[:], [[0, 1]], 0, 2).then_inc(sem.iota, 1)
+    v.memset(T.odd[:], 0.0).then_inc(sem.zero, 1)
+    v.wait_ge(sem.iota, 1)
+    v.tensor_scalar(T.pj[:], T.pi[:], 2, None, AluOpType.bitwise_and).then_inc(sem.par, 1)
+    v.wait_ge(sem.par, 1)
+    v.tensor_copy(T.par[:], T.pj[:]).then_inc(sem.par, 1)
+    v.wait_ge(sem.par, 2)
+
+    def cast(o, i, sm):
+        v.tensor_scalar(o, i, 4.0, T.par[:], AluOpType.mult, AluOpType.add).then_inc(sm, 1)
+
+    v.wait_ge(sem.ld_cw, 32)
+    cast(T.l0[:], T.cwi[:, :, L * servers[0]:L * servers[0] + L], sem.c0)
+    for u in range(2):
+        cast(T.lu[:, :, L * u:L * u + L], T.cwi[:, u, :], sem.cast)
+    cast(T.lo[:], T.cwi[:, :, L * rank:L * rank + L], sem.co)
+    g.wait_ge(sem.c0, 1)
     for c, (i, j) in enumerate(lists):
         es = list_engs(c, j - i)
         parts = []
         for k in range(i, j):
-            s = servers[k]
-            parts.append((s, T.lu[:, L * s:L * s + L], T.off[:, L * k:L * k + L], sem["lst%d" % k], es[k - i]))
+            src = T.l0[:] if k == 0 else T.lu[:, servers[k], :]
+            parts.append((servers[k], src, T.off[:, W * k:W * k + W], sem["lst%d" % k], es[k - i]))
         fused(parts)
+        if c == 0:
+            g.wait_ge(sem.cast, 2)
         if c == CFG["go"]:
             g.sem_inc(sem.go, 1)
 
-    def copy(q, o, i, sm):
+    def gather(q, kind, buf, u0, u1, offs, sm):
+        e, win = (0, T.bks) if kind == "a" else (1, T.odd)
+        o, i = buf[:, 64 * u0 + e:64 * u1:2], win[:, 0:4 * S].indirect(offs)
         if q is v:
             v.tensor_copy(o, i).then_inc(sm, 1)
         else:
             a.activation(o, i, COPY).then_inc(sm, 1)
 
-    both = ((v, (0, 1)), (a, (2, 3)))
-    for q, ts in both:
-        q.wait_ge(sem.ld_bk, 16)
-        for t in ts:
-            copy(q, T.win[:, S * t:S * t + S], T.bks[:, t:4 * S:4], sem.winv if q is v else sem.wins)
+    v.wait_ge(sem.ld_bk, 16)
+    v.wait_ge(sem.zero, 1)
+    v.tensor_copy(T.odd[:, 0:4 * S:2], T.bks[:, 1:4 * S:2]).then_inc(sem.odd, 1)
+    a.wait_ge(sem.ld_bk, 16)
+    a.wait_ge(sem.co, 1)
+    gather(a, "a", T.ho, 0, U, T.lo[:], sem.own)
+    a.wait_ge(sem.odd, 1)
+    gather(a, "b", T.ho, 0, U, T.lo[:], sem.own)
 
-    def gather(q, t, buf, c0, n, offs, sm):
-        copy(q, buf[:, 4 * c0 + t:4 * (c0 + n):4], T.win[:, S * t:S * t + S].indirect(offs), sm)
+    def quant_x(s):
+        v.wait_ge(sem["ld_x%d" % [p <= s < q for p, q in xl].index(True)], 16)
+        b0, b1 = S * s, S * (s + 1)
+        v.quantize_mx(T.xq[:, b0:b1], T.xsc[:, b0:b1], T.xs[:, 4 * b0:4 * b1]).then_inc(sem["xqd%d" % s], 1)
 
-    own = T.lu[:, L * rank:L * rank + L]
-    v.wait_ge(sem.winv, 2)
-    v.wait_ge(sem.cast, 1)
-    a.wait_ge(sem.wins, 2)
-    a.wait_ge(sem.cast, 1)
-    for q, ts in both:
-        for t in ts:
-            gather(q, t, T.ho, 0, S, own, sem.ownv if q is v else sem.owns)
-    v.wait_ge(sem.ownv, 2)
-    v.wait_ge(sem.owns, 2)
-    v.quantize_mx(T.oq[:], T.osc[:], T.ho[:]).then_inc(sem.ownq, 1)
+    order = [rank] + servers
+    early = [s for s in order if s < xl[CFG["nl"] - 1][1]][:CFG["nq"]]
+    late = [s for s in order if s not in early]
+    for s in early:
+        quant_x(s)
 
-    def quant_x(i):
-        for k in range(len(xl)):
-            if xl[k][0] < xq[i][1] and xq[i][0] < xl[k][1]:
-                v.wait_ge(sem["ld_x%d" % k], 16)
-        b0, b1 = S * xq[i][0], S * xq[i][1]
-        v.quantize_mx(T.xq[:, b0:b1], T.xsc[:, b0:b1], T.xs[:, 4 * b0:4 * b1]).then_inc(sem["xqd%d" % i], 1)
-
-    for i in range(CFG["nq"]):
-        quant_x(i)
-
-    def copies(q, i, ts):
-        k0, k1 = rounds[i]
-        for k in range(k0, k1):
+    def copies(q, n, op):
+        kind, u0, u1 = op
+        for k in range(u0 // U, (u1 - 1) // U + 1):
             q.wait_ge(sem["lst%d" % k], list_count(k))
-        for t in ts:
-            gather(q, t, T.h, S * k0, S * (k1 - k0), T.off[:, L * k0:L * k1], sem["gv%d" % i] if q is v else sem["gs%d" % i])
+        gather(q, kind, T.h, u0, u1, T.off[:, 2 * u0:2 * u1], sem[("gv%d" if q is v else "gs%d") % n])
 
     def send(ks, src, dv, coded):
         es = split(engs, len(ks))
@@ -178,44 +195,37 @@ def rank_program(g, core, T, topo):
             parts.append((mine[k], x, z, sem["arr%d" % rank], e))
         fused(parts)
 
-    a.wait_ge(sem.winv, 2)
-    v.wait_ge(sem.wins, 2)
-    begun = 0
-    for i, (k0, k1) in enumerate(rounds):
-        nv = CFG["vs"][i]
-        copies(a, i, range(nv, 4))
-        copies(v, i, range(begun, nv))
-        begun = CFG["ahead"][i]
-        if begun:
-            copies(v, i + 1, range(begun))
-        v.wait_ge(sem["gv%d" % i], nv)
-        v.wait_ge(sem["gs%d" % i], 4 - nv)
-        for m, (j0, j1) in enumerate(sends):
-            if not k0 <= j0 < k1:
-                continue
-            qd = sem["qd%d" % m]
-            c0, c1 = S * j0, S * j1
-            v.quantize_mx(T.sq[:, c0:c1], T.ss[:, c0:c1], T.h[:, 4 * c0:4 * c1]).then_inc(qd, 1)
-            g.wait_ge(qd, 1)
-            send(codes[m], T.sq, T.rq, True)
-            if scales[m]:
-                send(scales[m], T.ss, T.rs, False)
+    for n, op in enumerate(CFG["sca"]):
+        copies(a, n, op)
+    for n, op in enumerate(CFG["vec"]):
+        if op[0] != "q":
+            copies(v, n, op)
+            continue
+        k = op[1]
+        for name, ops in (("gv%d", CFG["vec"]), ("gs%d", CFG["sca"])):
+            for m, o in enumerate(ops):
+                if o[0] != "q" and o[1] < U * (k + 1) and U * k < o[2]:
+                    v.wait_ge(sem[name % m], 1)
+        qd = sem["qd%d" % k]
+        c0, c1 = S * k, S * (k + 1)
+        v.quantize_mx(T.sq[:, c0:c1], T.ss[:, c0:c1], T.h[:, 4 * c0:4 * c1]).then_inc(qd, 1)
+        g.wait_ge(qd, 1)
+        send(codes[k], T.sq, T.rq, True)
+        if scales[k]:
+            send(scales[k], T.ss, T.rs, False)
 
-    for i in range(CFG["nq"], len(xq)):
-        quant_x(i)
+    v.wait_ge(sem.own, 2)
+    v.quantize_mx(T.oq[:], T.osc[:], T.ho[:]).then_inc(sem.ownq, 1)
+    for s in late:
+        quant_x(s)
 
     def tile(b, s):
         return b[:, S * s:S * s + S]
 
-    def part(s):
-        return [p <= s < q for p, q in xq].index(True)
-
-    def arrival(s):
-        return [place(s, rank) in ks for ks in scales].index(True) if s != rank else 0
-
-    seq = sorted(range(N), key=lambda s: (arrival(s), part(s)))
+    ready = [s for s in early if s != rank] + [s for s in early if s == rank] + late
+    seq = [s for s in ready if s not in servers[-2:]] + servers[-2:]
     for i, s in enumerate(seq):
-        te.wait_ge(sem["xqd%d" % part(s)], 1)
+        te.wait_ge(sem["xqd%d" % s], 1)
         if s == rank:
             te.wait_ge(sem.ownq, 1)
             w, ws = T.oq[:], T.osc[:]
@@ -227,8 +237,9 @@ def rank_program(g, core, T, topo):
             mm.then_inc(sem.mm, 1)
 
     a.wait_ge(sem.mm, 1)
-    a.activation(T.yo[:], T.ps[:, 0:S], COPY).then_inc(sem.yc, 1)
-    a.wait_ge(sem.yc, 1)
+    for u in range(2):
+        a.activation(T.yo[:, u:S:2], T.ps[:, S // 2 * u:S // 2 * (u + 1)], COPY).then_inc(sem.yc, 1)
+    a.wait_ge(sem.yc, 2)
     a.dma_start(T.y[:], T.yo[:]).then_inc(sem.st, 16)
     a.wait_ge(sem.st, 16)
     g.wait_ge(sem.sent, left[0])

@@ -7,16 +7,19 @@ L = S // 16
 W = 2 * L
 U = 8
 CFG = dict(cols=[(2, 0), (1, 0), (2, 1), (1, 1), (0, 1)],
-           vec=[("a", 0, 8), ("a", 8, 16), ("q", 0), ("a", 16, 24), ("q", 1), ("a", 24, 30), ("q", 2),
-                ("a", 35, 40), ("q", 3), ("q", 4)],
-           sca=[("b", 0, 8), ("b", 8, 16), ("b", 16, 32), ("a", 30, 35), ("b", 32, 40)],
-           sc=[[0], [1], [2], [3], [4]], lc=[1, 2, 2], e1=8, xl=[4, 2], nl=1, nq=2, go=1)
+           vec=[("a", 0, 8), ("a", 8, 16), ("q", 0), ("b", 19, 26), ("q", 1), ("c",), ("b", 26, 32), ("q", 2),
+                ("a", 34, 40), ("q", 3), ("x",), ("q", 4)],
+           sca=[("b", 0, 8), ("b", 8, 19), ("a", 16, 26), ("a", 26, 34), ("b", 32, 40)],
+           sc=[[], [0, 1], [2], [3], [4]], lc=[1, 1, 2], le=[(0, 2), (0, 2), (0, 2), (3, 4), (1, 16)],
+           nl=2, go=0)
 
 SCRATCH = {
     "cwi": ("sbuf", [128, 2, N * L], "int32"),
     "pi": ("sbuf", [128, 1], "int32"),
     "pj": ("sbuf", [128, 1], "int32"),
     "par": ("sbuf", [128, 1], "float32"),
+    "raw": ("sbuf", [128, L], "int32"),
+    "rsrc": ("sbuf", [128, L], "int32"),
     "l0": ("sbuf", [128, W], "uint16"),
     "lo": ("sbuf", [128, W], "uint16"),
     "lu": ("sbuf", [128, N, W], "uint16"),
@@ -38,7 +41,7 @@ SCRATCH = {
     "ps": ("psum", [128, 512], "float32"),
 }
 SEMAPHORES = (["ld_cw", "ld_bk", "iota", "par", "zero", "c0", "cast", "co", "go", "odd", "own", "ownq", "mm", "yc", "st",
-               "sent"]
+               "sent", "cl", "ld_r", "half"]
               + ["ld_x%d" % k for k in range(N)] + ["xqd%d" % k for k in range(N)]
               + ["lst%d" % k for k in range(N)] + ["arr%d" % k for k in range(N)]
               + ["gv%d" % k for k in range(12)] + ["gs%d" % k for k in range(12)] + ["qd%d" % k for k in range(N)])
@@ -76,7 +79,6 @@ def rank_program(g, core, T, topo):
 
     lists = edges(CFG["lc"])
     codes, scales = [[k] for k in range(N - 1)], CFG["sc"]
-    xl = edges(CFG["xl"])
     mine = serves(rank)
 
     def dst(r):
@@ -89,13 +91,13 @@ def rank_program(g, core, T, topo):
     servers = sorted([s for s in range(N) if s != rank], key=lambda s: place(s, rank))
     engs = topo.engines(core, cores[mine[0]])
 
-    def list_engs(c, n):
-        return split(engs[::len(engs) // CFG["e1"]] if c == 0 else engs, n)
+    xl = [(servers[0] // 2 * 2, servers[0] // 2 * 2 + 2), (servers[1], servers[1] + 1), (servers[3], servers[3] + 1),
+          (rank // 2 * 2, rank // 2 * 2 + 2)]
+    lengs = [engs[i::n] for i, n in CFG["le"]]
+    hengs = ([e for e in engs if not any(e in es for es in lengs)] + engs[:1])[:4]
 
     def list_count(k):
-        for c, (i, j) in enumerate(lists):
-            if i <= k < j:
-                return len(list_engs(c, j - i)[k - i])
+        return len(lengs[k])
 
     def arr_count(k):
         return sum(len(split(engs, len(ks))[ks.index(k)]) for ks in codes + scales if k in ks)
@@ -103,6 +105,12 @@ def rank_program(g, core, T, topo):
     left = [0]
 
     def fused(parts):
+        if len(parts) == 1:
+            r, src, dv, sm, es = parts[0]
+            rid, pid, _ = topo.addr(cores[r])
+            left[0] += len(es)
+            g.remote_dma(dv, src, sm, sem.sent, pid, rid, bits(es))
+            return
         tr = []
         for r, src, dv, sm, es in parts:
             tr.append(RemoteDMATransfer(dst_ids=[dst(r)], dma_engine_mask=bits(es), remote_sem=sm, src=src, dst=dv))
@@ -113,9 +121,11 @@ def rank_program(g, core, T, topo):
         b0, b1 = 4 * S * xl[i][0], 4 * S * xl[i][1]
         sy.dma_start(T.xs[:, b0:b1], T.x[:, b0:b1]).then_inc(sem["ld_x%d" % i], 16)
 
-    sy.dma_start(T.cwi[0:128:2], T.cw[:]).then_inc(sem.ld_cw, 16)
-    a.dma_start(T.cwi[1:128:2], T.cw[:]).then_inc(sem.ld_cw, 16)
-    sy.dma_start(T.bks[:], T.bk[:]).then_inc(sem.ld_bk, 16)
+    last = N - 2
+    for t, q in enumerate((sy, a)):
+        q.dma_start(T.rsrc[t:128:2, :], T.cw[1:128:2, L * servers[last]:L * servers[last] + L]).then_inc(sem.ld_r, 16)
+        q.dma_start(T.cwi[t:128:2], T.cw[:]).then_inc(sem.ld_cw, 16)
+    a.dma_start(T.bks[:], T.bk[:]).then_inc(sem.ld_bk, 16)
     for i in range(CFG["nl"]):
         load_x(i)
     sy.wait_ge(sem.go, 1)
@@ -135,25 +145,24 @@ def rank_program(g, core, T, topo):
 
     v.wait_ge(sem.ld_cw, 32)
     cast(T.l0[:], T.cwi[:, :, L * servers[0]:L * servers[0] + L], sem.c0)
+    cast(T.lo[:], T.cwi[:, :, L * rank:L * rank + L], sem.co)
     for u in range(2):
         cast(T.lu[:, :, L * u:L * u + L], T.cwi[:, u, :], sem.cast)
-    cast(T.lo[:], T.cwi[:, :, L * rank:L * rank + L], sem.co)
+    g.wait_ge(sem.ld_r, 32)
+    fused([(servers[last], T.rsrc[:], T.raw[:], sem["lst%d" % last], lengs[last])])
     g.wait_ge(sem.c0, 1)
     for c, (i, j) in enumerate(lists):
-        es = list_engs(c, j - i)
-        parts = []
-        for k in range(i, j):
-            src = T.l0[:] if k == 0 else T.lu[:, servers[k], :]
-            parts.append((servers[k], src, T.off[:, W * k:W * k + W], sem["lst%d" % k], es[k - i]))
-        fused(parts)
+        fused([(servers[k], T.lu[:, servers[k], :] if k else T.l0[:], T.off[:, W * k:W * k + W], sem["lst%d" % k], lengs[k])
+               for k in range(i, j)])
         if c == 0:
             g.wait_ge(sem.cast, 2)
         if c == CFG["go"]:
             g.sem_inc(sem.go, 1)
+    fused([(servers[last], T.lu[:, servers[last], 0:L], T.off[:, W * last:W * last + L], sem.half, hengs)])
 
     def gather(q, kind, buf, u0, u1, offs, sm):
-        e, win = (0, T.bks) if kind == "a" else (1, T.odd)
-        o, i = buf[:, 64 * u0 + e:64 * u1:2], win[:, 0:4 * S].indirect(offs)
+        e, step = ("ab".index(kind), 2) if kind in "ab" else (int(kind), 4)
+        o, i = buf[:, 64 * u0 + e:64 * u1:step], (T.bks, T.odd)[e % 2][:, 0:4 * S].indirect(offs)
         if q is v:
             v.tensor_copy(o, i).then_inc(sm, 1)
         else:
@@ -166,23 +175,30 @@ def rank_program(g, core, T, topo):
     a.wait_ge(sem.co, 1)
     gather(a, "a", T.ho, 0, U, T.lo[:], sem.own)
     a.wait_ge(sem.odd, 1)
-    gather(a, "b", T.ho, 0, U, T.lo[:], sem.own)
+    gather(a, "b", T.ho, 0, U // 2, T.lo[:, 0:L], sem.own)
+    v.wait_ge(sem.odd, 1)
+    v.wait_ge(sem.co, 1)
+    gather(v, "b", T.ho, U // 2, U, T.lo[:, L:W], sem.own)
 
     def quant_x(s):
         v.wait_ge(sem["ld_x%d" % [p <= s < q for p, q in xl].index(True)], 16)
         b0, b1 = S * s, S * (s + 1)
         v.quantize_mx(T.xq[:, b0:b1], T.xsc[:, b0:b1], T.xs[:, 4 * b0:4 * b1]).then_inc(sem["xqd%d" % s], 1)
 
-    order = [rank] + servers
-    early = [s for s in order if s < xl[CFG["nl"] - 1][1]][:CFG["nq"]]
-    late = [s for s in order if s not in early]
+    early = [servers[0], servers[2]]
+    late = [rank, servers[3], servers[4]]
     for s in early:
         quant_x(s)
 
     def copies(q, n, op):
         kind, u0, u1 = op
         for k in range(u0 // U, (u1 - 1) // U + 1):
-            q.wait_ge(sem["lst%d" % k], list_count(k))
+            if k == last:
+                q.wait_ge(sem.half, len(hengs))
+                if u1 > U * last + U // 2:
+                    q.wait_ge(sem.cl, 1)
+            else:
+                q.wait_ge(sem["lst%d" % k], list_count(k))
         gather(q, kind, T.h, u0, u1, T.off[:, 2 * u0:2 * u1], sem[("gv%d" if q is v else "gs%d") % n])
 
     def send(ks, src, dv, coded):
@@ -198,13 +214,20 @@ def rank_program(g, core, T, topo):
     for n, op in enumerate(CFG["sca"]):
         copies(a, n, op)
     for n, op in enumerate(CFG["vec"]):
+        if op[0] == "c":
+            v.wait_ge(sem["lst%d" % last], list_count(last))
+            cast(T.off[:, W * last + L:W * last + W], T.raw[:], sem.cl)
+            continue
+        if op[0] == "x":
+            quant_x(servers[1])
+            continue
         if op[0] != "q":
             copies(v, n, op)
             continue
         k = op[1]
         for name, ops in (("gv%d", CFG["vec"]), ("gs%d", CFG["sca"])):
             for m, o in enumerate(ops):
-                if o[0] != "q" and o[1] < U * (k + 1) and U * k < o[2]:
+                if o[0] in "ab0123" and o[1] < U * (k + 1) and U * k < o[2]:
                     v.wait_ge(sem[name % m], 1)
         qd = sem["qd%d" % k]
         c0, c1 = S * k, S * (k + 1)
@@ -214,16 +237,16 @@ def rank_program(g, core, T, topo):
         if scales[k]:
             send(scales[k], T.ss, T.rs, False)
 
-    v.wait_ge(sem.own, 2)
-    v.quantize_mx(T.oq[:], T.osc[:], T.ho[:]).then_inc(sem.ownq, 1)
     for s in late:
+        if s == rank:
+            v.wait_ge(sem.own, 3)
+            v.quantize_mx(T.oq[:], T.osc[:], T.ho[:]).then_inc(sem.ownq, 1)
         quant_x(s)
 
     def tile(b, s):
         return b[:, S * s:S * s + S]
 
-    ready = [s for s in early if s != rank] + [s for s in early if s == rank] + late
-    seq = [s for s in ready if s not in servers[-2:]] + servers[-2:]
+    seq = early + [servers[1]] + late
     for i, s in enumerate(seq):
         te.wait_ge(sem["xqd%d" % s], 1)
         if s == rank:
@@ -236,10 +259,10 @@ def rank_program(g, core, T, topo):
         if i == N - 1:
             mm.then_inc(sem.mm, 1)
 
-    a.wait_ge(sem.mm, 1)
+    v.wait_ge(sem.mm, 1)
     for u in range(2):
-        a.activation(T.yo[:, u:S:2], T.ps[:, S // 2 * u:S // 2 * (u + 1)], COPY).then_inc(sem.yc, 1)
-    a.wait_ge(sem.yc, 2)
-    a.dma_start(T.y[:], T.yo[:]).then_inc(sem.st, 16)
-    a.wait_ge(sem.st, 16)
+        v.tensor_copy(T.yo[:, u:S:2], T.ps[:, S // 2 * u:S // 2 * (u + 1)]).then_inc(sem.yc, 1)
+    sy.wait_ge(sem.yc, 2)
+    sy.dma_start(T.y[:], T.yo[:]).then_inc(sem.st, 16)
+    sy.wait_ge(sem.st, 16)
     g.wait_ge(sem.sent, left[0])

from concourse.bass import DstId, RemoteDMATransfer
from concourse.mybir import dt, ActivationFunctionType, AluOpType

N = 6
S = 128
L = S // 16
W = 2 * L
U = 8
CFG = dict(cols=[(2, 0), (1, 0), (2, 1), (1, 1), (0, 1)],
           vec=[("a", 0, 8), ("a", 8, 16), ("q", 0), ("b", 19, 26), ("q", 1), ("c",), ("b", 26, 32), ("q", 2),
                ("a", 34, 40), ("q", 3), ("x",), ("q", 4)],
           sca=[("b", 0, 8), ("b", 8, 19), ("a", 16, 26), ("a", 26, 34), ("b", 32, 40)],
           sc=[[], [0, 1], [2], [3], [4]], lc=[1, 1, 2], le=[(0, 2), (0, 2), (0, 2), (3, 4), (1, 16)],
           nl=2, go=0)

SCRATCH = {
    "cwi": ("sbuf", [128, 2, N * L], "int32"),
    "pi": ("sbuf", [128, 1], "int32"),
    "pj": ("sbuf", [128, 1], "int32"),
    "par": ("sbuf", [128, 1], "float32"),
    "raw": ("sbuf", [128, L], "int32"),
    "rsrc": ("sbuf", [128, L], "int32"),
    "l0": ("sbuf", [128, W], "uint16"),
    "lo": ("sbuf", [128, W], "uint16"),
    "lu": ("sbuf", [128, N, W], "uint16"),
    "off": ("sbuf", [128, (N - 1) * W], "uint16"),
    "bks": ("sbuf", [128, 4 * S], "bfloat16"),
    "odd": ("sbuf", [128, 4 * S], "bfloat16"),
    "h": ("sbuf", [128, 4 * S * (N - 1)], "bfloat16"),
    "ho": ("sbuf", [128, 4 * S], "bfloat16"),
    "xs": ("sbuf", [128, 4 * S * N], "bfloat16"),
    "sq": ("sbuf", [128, S * (N - 1)], "float8_e4m3fn_x4"),
    "ss": ("sbuf", [128, S * (N - 1)], "uint8"),
    "oq": ("sbuf", [128, S], "float8_e4m3fn_x4"),
    "osc": ("sbuf", [128, S], "uint8"),
    "rq": ("sbuf", [128, S * N], "float8_e4m3fn_x4"),
    "rs": ("sbuf", [128, S * N], "uint8"),
    "xq": ("sbuf", [128, S * N], "float8_e4m3fn_x4"),
    "xsc": ("sbuf", [128, S * N], "uint8"),
    "yo": ("sbuf", [128, S], "float32"),
    "ps": ("psum", [128, 512], "float32"),
}
SEMAPHORES = (["ld_cw", "ld_bk", "iota", "par", "zero", "c0", "cast", "co", "go", "odd", "own", "ownq", "mm", "yc", "st",
               "sent", "cl", "ld_r", "half"]
              + ["ld_x%d" % k for k in range(N)] + ["xqd%d" % k for k in range(N)]
              + ["lst%d" % k for k in range(N)] + ["arr%d" % k for k in range(N)]
              + ["gv%d" % k for k in range(12)] + ["gs%d" % k for k in range(12)] + ["qd%d" % k for k in range(N)])


def edges(ns):
    return [(sum(ns[:i]), sum(ns[:i + 1])) for i in range(len(ns))]


def serves(s):
    return [2 * ((s // 2 + d) % (N // 2)) + (s + f) % 2 for d, f in CFG["cols"]]


def split(engs, k):
    if k == 3:
        return [engs[0::4], engs[2::4], engs[1::2]]
    return [engs[i::k] for i in range(k)]


def bits(es):
    m = 0
    for e in es:
        m |= 1 << e
    return m


def rank_program(g, core, T, topo):
    rank = T.rank_of(core)
    if rank is None:
        return
    cores = T.cores
    sem = T.sem
    v, a, te, sy = g.vector, g.scalar, g.tensor, g.sync
    COPY = ActivationFunctionType.Copy

    lists = edges(CFG["lc"])
    codes, scales = [[k] for k in range(N - 1)], CFG["sc"]
    mine = serves(rank)

    def dst(r):
        rid, pid, _ = topo.addr(cores[r])
        return DstId(rid=rid, pnc=pid)

    def place(s, r):
        return serves(s).index(r)

    servers = sorted([s for s in range(N) if s != rank], key=lambda s: place(s, rank))
    engs = topo.engines(core, cores[mine[0]])

    xl = [(servers[0] // 2 * 2, servers[0] // 2 * 2 + 2), (servers[1], servers[1] + 1), (servers[3], servers[3] + 1),
          (rank // 2 * 2, rank // 2 * 2 + 2)]
    lengs = [engs[i::n] for i, n in CFG["le"]]
    hengs = ([e for e in engs if not any(e in es for es in lengs)] + engs[:1])[:4]

    def list_count(k):
        return len(lengs[k])

    def arr_count(k):
        return sum(len(split(engs, len(ks))[ks.index(k)]) for ks in codes + scales if k in ks)

    left = [0]

    def fused(parts):
        if len(parts) == 1:
            r, src, dv, sm, es = parts[0]
            rid, pid, _ = topo.addr(cores[r])
            left[0] += len(es)
            g.remote_dma(dv, src, sm, sem.sent, pid, rid, bits(es))
            return
        tr = []
        for r, src, dv, sm, es in parts:
            tr.append(RemoteDMATransfer(dst_ids=[dst(r)], dma_engine_mask=bits(es), remote_sem=sm, src=src, dst=dv))
            left[0] += len(es)
        g.remote_dma_fused(tr, local_sem=sem.sent)

    def load_x(i):
        b0, b1 = 4 * S * xl[i][0], 4 * S * xl[i][1]
        sy.dma_start(T.xs[:, b0:b1], T.x[:, b0:b1]).then_inc(sem["ld_x%d" % i], 16)

    last = N - 2
    for t, q in enumerate((sy, a)):
        q.dma_start(T.rsrc[t:128:2, :], T.cw[1:128:2, L * servers[last]:L * servers[last] + L]).then_inc(sem.ld_r, 16)
        q.dma_start(T.cwi[t:128:2], T.cw[:]).then_inc(sem.ld_cw, 16)
    a.dma_start(T.bks[:], T.bk[:]).then_inc(sem.ld_bk, 16)
    for i in range(CFG["nl"]):
        load_x(i)
    sy.wait_ge(sem.go, 1)
    for i in range(CFG["nl"], len(xl)):
        load_x(i)

    g.iota(T.pi[:], [[0, 1]], 0, 2).then_inc(sem.iota, 1)
    v.memset(T.odd[:], 0.0).then_inc(sem.zero, 1)
    v.wait_ge(sem.iota, 1)
    v.tensor_scalar(T.pj[:], T.pi[:], 2, None, AluOpType.bitwise_and).then_inc(sem.par, 1)
    v.wait_ge(sem.par, 1)
    v.tensor_copy(T.par[:], T.pj[:]).then_inc(sem.par, 1)
    v.wait_ge(sem.par, 2)

    def cast(o, i, sm):
        v.tensor_scalar(o, i, 4.0, T.par[:], AluOpType.mult, AluOpType.add).then_inc(sm, 1)

    v.wait_ge(sem.ld_cw, 32)
    cast(T.l0[:], T.cwi[:, :, L * servers[0]:L * servers[0] + L], sem.c0)
    cast(T.lo[:], T.cwi[:, :, L * rank:L * rank + L], sem.co)
    for u in range(2):
        cast(T.lu[:, :, L * u:L * u + L], T.cwi[:, u, :], sem.cast)
    g.wait_ge(sem.ld_r, 32)
    fused([(servers[last], T.rsrc[:], T.raw[:], sem["lst%d" % last], lengs[last])])
    g.wait_ge(sem.c0, 1)
    for c, (i, j) in enumerate(lists):
        fused([(servers[k], T.lu[:, servers[k], :] if k else T.l0[:], T.off[:, W * k:W * k + W], sem["lst%d" % k], lengs[k])
               for k in range(i, j)])
        if c == 0:
            g.wait_ge(sem.cast, 2)
        if c == CFG["go"]:
            g.sem_inc(sem.go, 1)
    fused([(servers[last], T.lu[:, servers[last], 0:L], T.off[:, W * last:W * last + L], sem.half, hengs)])

    def gather(q, kind, buf, u0, u1, offs, sm):
        e, step = ("ab".index(kind), 2) if kind in "ab" else (int(kind), 4)
        o, i = buf[:, 64 * u0 + e:64 * u1:step], (T.bks, T.odd)[e % 2][:, 0:4 * S].indirect(offs)
        if q is v:
            v.tensor_copy(o, i).then_inc(sm, 1)
        else:
            a.activation(o, i, COPY).then_inc(sm, 1)

    v.wait_ge(sem.ld_bk, 16)
    v.wait_ge(sem.zero, 1)
    v.tensor_copy(T.odd[:, 0:4 * S:2], T.bks[:, 1:4 * S:2]).then_inc(sem.odd, 1)
    a.wait_ge(sem.ld_bk, 16)
    a.wait_ge(sem.co, 1)
    gather(a, "a", T.ho, 0, U, T.lo[:], sem.own)
    a.wait_ge(sem.odd, 1)
    gather(a, "b", T.ho, 0, U // 2, T.lo[:, 0:L], sem.own)
    v.wait_ge(sem.odd, 1)
    v.wait_ge(sem.co, 1)
    gather(v, "b", T.ho, U // 2, U, T.lo[:, L:W], sem.own)

    def quant_x(s):
        v.wait_ge(sem["ld_x%d" % [p <= s < q for p, q in xl].index(True)], 16)
        b0, b1 = S * s, S * (s + 1)
        v.quantize_mx(T.xq[:, b0:b1], T.xsc[:, b0:b1], T.xs[:, 4 * b0:4 * b1]).then_inc(sem["xqd%d" % s], 1)

    early = [servers[0], servers[2]]
    late = [rank, servers[3], servers[4]]
    for s in early:
        quant_x(s)

    def copies(q, n, op):
        kind, u0, u1 = op
        for k in range(u0 // U, (u1 - 1) // U + 1):
            if k == last:
                q.wait_ge(sem.half, len(hengs))
                if u1 > U * last + U // 2:
                    q.wait_ge(sem.cl, 1)
            else:
                q.wait_ge(sem["lst%d" % k], list_count(k))
        gather(q, kind, T.h, u0, u1, T.off[:, 2 * u0:2 * u1], sem[("gv%d" if q is v else "gs%d") % n])

    def send(ks, src, dv, coded):
        es = split(engs, len(ks))
        parts = []
        for e, k in zip(es, ks):
            x, z = src[:, S * k:S * k + S], dv[:, S * rank:S * rank + S]
            if coded:
                x, z = x.bitcast(dt.uint8), z.bitcast(dt.uint8)
            parts.append((mine[k], x, z, sem["arr%d" % rank], e))
        fused(parts)

    for n, op in enumerate(CFG["sca"]):
        copies(a, n, op)
    for n, op in enumerate(CFG["vec"]):
        if op[0] == "c":
            v.wait_ge(sem["lst%d" % last], list_count(last))
            cast(T.off[:, W * last + L:W * last + W], T.raw[:], sem.cl)
            continue
        if op[0] == "x":
            quant_x(servers[1])
            continue
        if op[0] != "q":
            copies(v, n, op)
            continue
        k = op[1]
        for name, ops in (("gv%d", CFG["vec"]), ("gs%d", CFG["sca"])):
            for m, o in enumerate(ops):
                if o[0] in "ab0123" and o[1] < U * (k + 1) and U * k < o[2]:
                    v.wait_ge(sem[name % m], 1)
        qd = sem["qd%d" % k]
        c0, c1 = S * k, S * (k + 1)
        v.quantize_mx(T.sq[:, c0:c1], T.ss[:, c0:c1], T.h[:, 4 * c0:4 * c1]).then_inc(qd, 1)
        g.wait_ge(qd, 1)
        send(codes[k], T.sq, T.rq, True)
        if scales[k]:
            send(scales[k], T.ss, T.rs, False)

    for s in late:
        if s == rank:
            v.wait_ge(sem.own, 3)
            v.quantize_mx(T.oq[:], T.osc[:], T.ho[:]).then_inc(sem.ownq, 1)
        quant_x(s)

    def tile(b, s):
        return b[:, S * s:S * s + S]

    seq = early + [servers[1]] + late
    for i, s in enumerate(seq):
        te.wait_ge(sem["xqd%d" % s], 1)
        if s == rank:
            te.wait_ge(sem.ownq, 1)
            w, ws = T.oq[:], T.osc[:]
        else:
            te.wait_ge(sem["arr%d" % s], arr_count(place(s, rank)))
            w, ws = tile(T.rq, s), tile(T.rs, s)
        mm = te.matmul_mx(T.ps[:, 0:S], tile(T.xq, s), tile(T.xsc, s), w, ws, i == 0, i == N - 1)
        if i == N - 1:
            mm.then_inc(sem.mm, 1)

    v.wait_ge(sem.mm, 1)
    for u in range(2):
        v.tensor_copy(T.yo[:, u:S:2], T.ps[:, S // 2 * u:S // 2 * (u + 1)]).then_inc(sem.yc, 1)
    sy.wait_ge(sem.yc, 2)
    sy.dma_start(T.y[:], T.yo[:]).then_inc(sem.st, 16)
    sy.wait_ge(sem.st, 16)
    g.wait_ge(sem.sent, left[0])
